import numpy as np
import ml_dtypes


def mxq(x, axis, fmt="e4m3"):
    dtype, down = {"e4m3": (ml_dtypes.float8_e4m3fn, 7), "e5m2": (ml_dtypes.float8_e5m2, 14)}[fmt]
    v = np.moveaxis(np.asarray(x, np.float32).astype(ml_dtypes.bfloat16).astype(np.float64), axis, -1)
    blocks = v.reshape(v.shape[:-1] + (-1, 32))
    amax = np.abs(blocks).max(-1, keepdims=True)
    byte = np.maximum(np.where(amax > 0, np.frexp(amax)[1] - 1 + 127, 0) - down, 1)
    scale = np.exp2(byte - 127.0)
    codes = (blocks / scale).astype(np.float32).astype(dtype).astype(np.float64)
    return np.moveaxis((codes * scale).reshape(v.shape), -1, axis)


WIDE = False


def mx_kscale(k):
    if not WIDE:
        return np.ones(k)
    levels = np.array([10, -10, 5, -5, 0])
    if k % 512:
        return np.exp2(np.random.permutation(np.resize(levels, k // 32))).repeat(32)
    a = np.empty((k // 512, 16))
    for p in range(k // 512):
        a[p, :8] = np.random.permutation(np.resize(levels, 8))
        for g in range(8):
            far = levels[np.abs(levels - a[p, g]) >= 10]
            a[p, g + 8] = far[np.random.randint(len(far))]
    return np.exp2(a.ravel()).repeat(32)


def f64(x):
    return np.asarray(x).astype(np.float64)


def striped(idx):
    return np.tile(idx.reshape(-1, 16).T, (8, 1)).astype(np.uint16)


def unstriped(offs):
    return offs[:16].T.reshape(-1).astype(np.int64)


E2M1 = np.array([0.0, 0.5, 1.0, 1.5, 2.0, 3.0, 4.0, 6.0, -0.0, -0.5, -1.0, -1.5, -2.0, -3.0, -4.0, -6.0])


def pack_weight(w, fmt):
    k, n = w.shape
    w = f64(np.asarray(w, np.float32).astype(ml_dtypes.bfloat16)).reshape(k // 32, 32, n)
    amax = np.abs(w).max(1)
    if fmt == "e4m3":
        byte = np.frexp(amax)[1] - 1 + 127 - 7
    else:
        mant, ex = np.frexp(amax / 6.0)
        byte = np.where(mant > 0.5, ex, ex - 1) + 127
    byte = np.clip(np.where(amax > 0, byte, 1), 1, 254)
    scaled = (w * np.exp2(127.0 - byte)[:, None, :]).reshape(k, n).astype(np.float32)
    by_word = np.ascontiguousarray(scaled.reshape(k // 512, 128, 4, n).transpose(0, 1, 3, 2))
    if fmt == "e4m3":
        words = by_word.astype(ml_dtypes.float8_e4m3fn).view(np.uint8)
    else:
        c = by_word.astype(ml_dtypes.float4_e2m1fn).view(np.uint8) & 0xF
        words = (c[..., 0::2] | (c[..., 1::2] << 4)).reshape(k // 512, 128, 2 * n)
    return np.ascontiguousarray(words), np.ascontiguousarray(byte.astype(np.uint8).reshape(k // 512, 16, n))


def unpack_weight(words, scales, fmt):
    g, _, n = scales.shape
    words = np.ascontiguousarray(words).reshape(g, 128, n, -1)
    if fmt == "e4m3":
        vals = words.view(ml_dtypes.float8_e4m3fn).astype(np.float64)
    else:
        nib = np.empty((g, 128, n, 4), np.uint8)
        nib[..., 0::2] = words & 0xF
        nib[..., 1::2] = words >> 4
        vals = E2M1[nib]
    vals = vals * np.repeat(np.exp2(scales.astype(np.float64) - 127.0), 8, axis=1)[..., None]
    return vals.transpose(0, 1, 3, 2).reshape(g * 512, n)


def gelu(v):
    return 0.5 * v * (1.0 + np.tanh(np.sqrt(2.0 / np.pi) * (v + 0.044715 * v**3)))


K, KA, T, S, H, T2, P = 1024, 512, 2048, 512, 1536, 1024, 512

def setup_inputs():
    n = np.random.standard_normal
    s = mx_kscale(K)[:, None]
    u = mx_kscale(H)[:, None]
    d = {}
    d["tab_words"], d["tab_scales"] = pack_weight(n((K, T)) * s, "e4m3")
    d["offs"] = striped(np.random.permutation(T)[:S])
    d["offs2"] = striped(np.random.permutation(T2)[:S])
    d["offs3"] = striped(np.random.permutation(T2)[:P])
    w = 2.5 * n((K, H)) / K ** 0.5 / s
    d["w4_words"], d["w4_scales"] = pack_weight(w[:KA], "e2m1")
    d["w1"] = w[KA:].astype(np.float32)
    d["lotw"] = (2.0 * n((H, S)) * u).astype(np.float32)
    d["wgs"] = np.exp(0.3 * n((128, S))).astype(np.float32)
    d["page0"] = (n((H, T2)) * u).astype(np.float32)
    d["cleanm"] = (0.8 * n((H, P)) * u).astype(np.float32)
    sign = np.random.choice([-1.0, 1.0], H)
    d["gv"] = (sign * np.exp(0.3 * n(H)) / H ** 0.5 / u[:, 0] ** 2).astype(np.float32)
    d["slotv"] = n(T2).astype(np.float32)
    return d

def reference(tab_words, tab_scales, offs, offs2, offs3, w4_words, w4_scales, w1, lotw, wgs, page0, cleanm, gv, slotv):
    v = unpack_weight(tab_words, tab_scales, "e4m3")[:, unstriped(offs)]
    w4 = unpack_weight(w4_words, w4_scales, "e2m1")
    w1q = mxq(f64(w1), 0, "e4m3")
    a = w4.T @ v[:KA] + w1q.T @ v[KA:]
    h = f64(lotw) / (1.0 + np.abs(a))
    page = f64(page0).copy()
    page[:, unstriped(offs2)] = np.tile(f64(wgs), (H // 128, 1)) * h
    x = (page[:, unstriped(offs3)] + f64(cleanm)) * f64(gv)[:, None]
    e = mxq(page, 0, "e4m3").T @ mxq(x, 0, "e4m3")
    return np.abs(e - f64(slotv)[:, None])

@@ -1,0 +1,245 @@
+from contextlib import ExitStack
+
+import concourse.mybir as mybir
+
+F32 = mybir.dt.float32
+BF16 = mybir.dt.bfloat16
+I32 = mybir.dt.int32
+U32 = mybir.dt.uint32
+U16 = mybir.dt.uint16
+U8 = mybir.dt.uint8
+FP8X4 = mybir.dt.float8_e4m3fn_x4
+FP4X4 = mybir.dt.float4_e2m1fn_x4
+ACT = mybir.ActivationFunctionType
+ALU = mybir.AluOpType
+
+K, KA, T, S, H, T2, NP = 1024, 512, 2048, 512, 1536, 1024, 512
+P = 128
+PASSES = H // 512
+TILES = H // P
+FLOPS = 2 * K * H * S + 2 * H * T2 * NP
+AHEAD = 3
+
+
+def tile_list_cork_taint_deviation_kernel(
+    tc, tab_words, tab_scales, offs, offs2, offs3, w4_words, w4_scales, w1, lotw, wgs, page0, cleanm, gv, slotv, out
+):
+    nc = tc.nc
+    with ExitStack() as ctx:
+        keep = ctx.enter_context(tc.tile_pool(name="keep", bufs=1))
+        ring = ctx.enter_context(tc.tile_pool(name="ring", bufs=2))
+        psum = ctx.enter_context(tc.psum_pool(name="psum", bufs=1))
+
+        idx = keep.tile([P, S // 16], U16, name="idx")
+        idx2 = keep.tile([P, S // 16], U16, name="idx2")
+        idx3 = keep.tile([P, NP // 16], U16, name="idx3")
+        tab_w = [keep.tile([P, T], I32, name="tab_w%d" % (a)) for a in range(2)]
+        tab_s = keep.tile([P, T], U8, name="tab_s")
+        w4_raw = keep.tile([P, 2 * H], U8, name="w4_raw")
+        w4s_raw = keep.tile([P, H], U8, name="w4s_raw")
+        wgs_sb = keep.tile([P, 4, S], F32, name="wgs_sb")
+        gv_sb = keep.tile([P, PASSES, 4], F32, name="gv_sb")
+        slot_sb = keep.tile([P, T2 // P], F32, name="slot_sb")
+        warm = keep.tile([P, 1], F32, name="warm")
+        warm2 = keep.tile([P, 1], F32, name="warm2")
+
+        nc.vector.memset(tab_s[:].bitcast(I32), 0)
+        nc.vector.memset(w4s_raw[:].bitcast(I32), 0)
+        nc.vector.memset(warm[:], 1.0)
+        nc.scalar.activation(warm2[:], warm[:], ACT.Abs_reciprocal_sqrt)
+
+        w1_raw, lot_sb, page_sb, clean_sb = {}, {}, {}, {}
+
+        def load_w1(b):
+            w1_raw[b] = ring.tile([P, 4, 512], F32, name="w1_raw", bufs=2)
+            nc.sync.dma_start(w1_raw[b][:], w1.rearrange("(p j) r -> p j r", j=4)[:, :, 512 * b : 512 * (b + 1)])
+
+        def rows(src, k):
+            return src.rearrange("(b p t) c -> b t p c", p=P, t=4)[k // 4, k % 4]
+
+        def load_lot_page(k):
+            lot_sb[k] = ring.tile([P, S], F32, name="lot_sb", bufs=6)
+            nc.sync.dma_start(lot_sb[k][:], rows(lotw, k))
+            page_sb[k] = ring.tile([P, T2], F32, name="page_sb", bufs=8)
+            nc.sync.dma_start(page_sb[k][:], rows(page0, k))
+
+        def load_clean(k):
+            clean_sb[k] = ring.tile([P, NP], F32, name="clean_sb", bufs=6)
+            nc.sync.dma_start(clean_sb[k][:], rows(cleanm, k))
+
+        nc.sync.dma_start(idx[:], offs)
+        load_w1(0)
+        nc.sync.dma_start(tab_w[0][:], tab_words[0].rearrange("p t i -> p (t i)").bitcast(I32))
+        nc.sync.dma_start(w4_raw[:].bitcast(I32), w4_words[0].bitcast(I32))
+        for q in range(4):
+            nc.sync.dma_start(tab_s[32 * q : 32 * q + 8, :].bitcast(I32), tab_scales[:, 4 * q : 4 * q + 4, :].bitcast(I32))
+        nc.sync.dma_start(tab_w[1][:], tab_words[1].rearrange("p t i -> p (t i)").bitcast(I32))
+        for q in range(4):
+            nc.sync.dma_start(w4s_raw[32 * q : 32 * q + 4, :].bitcast(I32), w4_scales[0, 4 * q : 4 * q + 4, :].bitcast(I32))
+        for q in range(4):
+            nc.sync.dma_start(wgs_sb[32 * q : 32 * (q + 1)], wgs.rearrange("(p t) c -> p t c", t=4))
+        nc.sync.dma_start(idx2[:], offs2)
+        load_lot_page(0)
+        nc.sync.dma_start(idx3[:], offs3)
+        load_clean(0)
+        nc.sync.dma_start(gv_sb[:], gv.rearrange("(b p t) -> p b t", p=P, t=4))
+        load_lot_page(1)
+        load_clean(1)
+        load_w1(1)
+        for k in range(2, TILES):
+            load_lot_page(k)
+            load_clean(k)
+            if k == 4:
+                load_w1(2)
+        with nc.allow_non_contiguous_dma(reason="one offset a partition"):
+            nc.sync.dma_start(slot_sb[:], slotv.rearrange("(m p) -> p m", p=P))
+
+        w4_c = [keep.tile([P, 4, P, 2], U8, name="w4_c%d" % (b), align_bytes=64) for b in range(PASSES)]
+        w4_s = [keep.tile([P, 4, P], U8, name="w4_s%d" % (b), align_bytes=64) for b in range(PASSES)]
+        w1_c = [keep.tile([P, 512], U32, name="w1_c%d" % (b), align_bytes=64) for b in range(PASSES)]
+        w1_s = [keep.tile([P, 512], U8, name="w1_s%d" % (b), align_bytes=64) for b in range(PASSES)]
+        v_c = [keep.tile([P, S], U32, name="v_c%d" % (a), align_bytes=64) for a in range(2)]
+        v_s = keep.tile([P, S], U8, name="v_s", align_bytes=64)
+
+        def deal_w4_words(b):
+            nc.vector.tensor_copy(
+                w4_c[b][:], w4_raw[:, 1024 * b : 1024 * (b + 1)].rearrange("p (m t e) -> p t m e", t=4, e=2)
+            )
+
+        def deal_w4_scales(b):
+            nc.vector.tensor_copy(w4_s[b][:], w4s_raw[:, 512 * b : 512 * (b + 1)].rearrange("p (m t) -> p t m", t=4))
+
+        def weave_w1(b, copy):
+            woven = ring.tile([P, 4, P, 4], BF16, name="w1_woven", align_bytes=64)
+            copy(woven[:].rearrange("p t m j -> p m j t"), w1_raw[b][:].rearrange("p j (m t) -> p m j t", t=4))
+            return woven
+
+        def quant_w1(b, woven):
+            nc.vector.quantize_mx(w1_c[b][:].bitcast(FP8X4), w1_s[b][:], woven[:].rearrange("p t m j -> p (t m j)"))
+
+        a_ps, shrink = {}, {}
+
+        def readout(k):
+            b, t = divmod(k, 4)
+            a_ps[k] = psum.tile([P, S], F32, name="bank%d" % (k % 8))
+            cols = slice(P * t, P * (t + 1))
+            nc.tensor.matmul_mx(
+                a_ps[k][:], lhsT=w4_c[b][:, t].rearrange("p m e -> p (m e)").bitcast(FP4X4), lhsT_scale=w4_s[b][:, t],
+                rhs=v_c[0][:].bitcast(FP8X4), rhs_scale=v_s[:], start=True, stop=False,
+            )
+            nc.tensor.matmul_mx(
+                a_ps[k][:], lhsT=w1_c[b][:, cols].bitcast(FP8X4), lhsT_scale=w1_s[b][:, cols],
+                rhs=v_c[1][:].bitcast(FP8X4), rhs_scale=v_s[4:P, :], start=False, stop=True,
+            )
+
+        def chain(k):
+            shrink[k] = ring.tile([P, S], F32, name="shrink", bufs=AHEAD + 2)
+            nc.scalar.activation(shrink[k][:], a_ps[k][:], ACT.Abs)
+            nc.scalar.activation(shrink[k][:], shrink[k][:], ACT.Abs_reciprocal_sqrt, bias=1.0)
+            nc.scalar.activation(shrink[k][:], shrink[k][:], ACT.Square)
+
+        def weigh(k):
+            nc.vector.tensor_tensor(lot_sb[k][:], lot_sb[k][:], wgs_sb[:, k % 4, :], ALU.mult)
+
+        woven0 = weave_w1(0, nc.vector.tensor_copy)
+        deal_w4_words(0)
+        quant_w1(0, woven0)
+        nc.vector.tensor_copy(v_c[0][:], tab_w[0][:].bitcast(U32).indirect(idx[:]))
+        nc.vector.tensor_copy(v_s[:], tab_s[:].indirect(idx[:]))
+        deal_w4_words(1)
+        deal_w4_words(2)
+        deal_w4_scales(0)
+        nc.vector.tensor_copy(v_c[1][:], tab_w[1][:].bitcast(U32).indirect(idx[:]))
+        for k in range(4):
+            readout(k)
+        deal_w4_scales(1)
+        deal_w4_scales(2)
+        for k in range(AHEAD):
+            chain(k)
+        weigh(0)
+
+        page_c = [[keep.tile([P, 512], U32, name="page_c%d%d" % (b, h), align_bytes=64) for h in range(2)] for b in range(PASSES)]
+        page_s = [[keep.tile([P, 512], U8, name="page_s%d%d" % (b, h), align_bytes=64) for h in range(2)] for b in range(PASSES)]
+        x_c = [keep.tile([P, NP], U32, name="x_c%d" % (b), align_bytes=64) for b in range(PASSES)]
+        x_s = [keep.tile([P, NP], U8, name="x_s%d" % (b), align_bytes=64) for b in range(PASSES)]
+        e_ps = {}
+
+        def weave(dst, src, slots):
+            nc.scalar.copy(
+                dst[:].rearrange("p (c i) t -> p c t i", i=4)[:, :, 0:slots, :],
+                src.rearrange("p t (c i) -> p c t i", i=4)[:, :, 0:slots, :],
+            )
+
+        def scores(b, page_woven, x_woven):
+            for h in range(2):
+                nc.vector.quantize_mx(
+                    page_c[b][h][:].bitcast(FP8X4), page_s[b][h][:], page_woven[h][:].rearrange("p c t -> p (c t)")
+                )
+            nc.vector.quantize_mx(x_c[b][:].bitcast(FP8X4), x_s[b][:], x_woven[:].rearrange("p c t -> p (c t)"))
+            for m in range(T2 // P):
+                if b == 0:
+                    e_ps[m] = psum.tile([P, NP], F32, name="bank%d" % (m))
+                cols = slice(P * (m % 4), P * (m % 4 + 1))
+                nc.tensor.matmul_mx(
+                    e_ps[m][:], lhsT=page_c[b][m // 4][:, cols].bitcast(FP8X4), lhsT_scale=page_s[b][m // 4][:, cols],
+                    rhs=x_c[b][:].bitcast(FP8X4), rhs_scale=x_s[b][:], start=(b == 0), stop=(b == PASSES - 1),
+                )
+
+        pending = []
+        for k in range(TILES):
+            b, t = divmod(k, 4)
+            last = b == PASSES - 1
+            if t == 0:
+                page_bf = ring.tile([P, 4, T2], BF16, name="page_bf")
+                x_bf = ring.tile([P, 4, NP], BF16, name="x_bf")
+                page_woven = [ring.tile([P, 512, 4], BF16, name="page_woven%d" % (h), align_bytes=64) for h in range(2)]
+                x_woven = ring.tile([P, NP, 4], BF16, name="x_woven", align_bytes=64)
+            if t == 0 and not last:
+                quant_w1(b + 1, weave_w1(b + 1, nc.scalar.copy))
+                for kk in range(4 * b + 4, 4 * b + 8):
+                    readout(kk)
+            nc.vector.tensor_tensor(page_sb[k][:].indirect(idx2[:]), shrink[k][:], lot_sb[k][:], ALU.mult)
+            if k + 1 < TILES:
+                weigh(k + 1)
+            shifted = ring.tile([P, NP], F32, name="shifted")
+            nc.vector.tensor_tensor(shifted[:], page_sb[k][:].indirect(idx3[:]), clean_sb[k][:], ALU.add)
+            if k + AHEAD < TILES:
+                chain(k + AHEAD)
+            gain = gv_sb[:, b, t : t + 1]
+            if not last:
+                nc.scalar.copy(page_bf[:, t, :], page_sb[k][:])
+                nc.scalar.activation(x_bf[:, t, :], shifted[:], ACT.Copy, scale=gain)
+                if t == 3:
+                    for h in range(2):
+                        weave(page_woven[h], page_bf[:, :, 512 * h : 512 * (h + 1)], 4)
+                    weave(x_woven, x_bf[:], 4)
+                    pending.append((b, page_woven, x_woven))
+            else:
+                if t < 2:
+                    nc.scalar.copy(page_bf[:, t, :], page_sb[k][:])
+                elif t == 2:
+                    nc.scalar.copy(page_bf[:, t, 0:512], page_sb[k][:, 0:512])
+                else:
+                    nc.scalar.copy(page_woven[0][:, :, t], page_sb[k][:, 0:512])
+                if t >= 2:
+                    nc.vector.tensor_copy(page_woven[1][:, :, t], page_sb[k][:, 512:1024])
+                if t == 1:
+                    weave(page_woven[1], page_bf[:, :, 512:1024], 2)
+                if t < 3:
+                    nc.scalar.activation(x_bf[:, t, :], shifted[:], ACT.Copy, scale=gain)
+                else:
+                    nc.scalar.activation(x_woven[:, :, t], shifted[:], ACT.Copy, scale=gain)
+                if t == 2:
+                    weave(page_woven[0], page_bf[:, :, 0:512], 3)
+                    weave(x_woven, x_bf[:], 3)
+                if t == 3:
+                    pending.append((b, page_woven, x_woven))
+            if pending and (t == 0 or k == TILES - 1):
+                for item in pending:
+                    scores(*item)
+                pending.clear()
+
+        for m in range(T2 // P):
+            staged = ring.tile([P, NP], F32, name="staged", bufs=4)
+            nc.scalar.activation(staged[:], e_ps[m][:], ACT.Abs, bias=slot_sb[:, m : m + 1], scale=-1.0)
+            nc.sync.dma_start(out[P * m : P * (m + 1), :], staged[:])

@@ -18,7 +18,7 @@ P = 128
 PASSES = H // 512
 TILES = H // P
 FLOPS = 2 * K * H * S + 2 * H * T2 * NP
-AHEAD = 3
+AHEAD = 5
 
 
 def tile_list_cork_taint_deviation_kernel(
@@ -43,7 +43,7 @@ def tile_list_cork_taint_deviation_kernel(
         warm = keep.tile([P, 1], F32, name="warm")
         warm2 = keep.tile([P, 1], F32, name="warm2")
 
-        nc.vector.memset(tab_s[:].bitcast(I32), 0)
+        nc.gpsimd.memset(tab_s[:].bitcast(I32), 0)
         nc.vector.memset(w4s_raw[:].bitcast(I32), 0)
         nc.vector.memset(warm[:], 1.0)
         nc.scalar.activation(warm2[:], warm[:], ACT.Abs_reciprocal_sqrt)
@@ -67,18 +67,18 @@ def tile_list_cork_taint_deviation_kernel(
             clean_sb[k] = ring.tile([P, NP], F32, name="clean_sb", bufs=6)
             nc.sync.dma_start(clean_sb[k][:], rows(cleanm, k))
 
+        for q in range(4):
+            nc.gpsimd.dma_start(tab_s[32 * q : 32 * q + 8, :].bitcast(I32), tab_scales[:, 4 * q : 4 * q + 4, :].bitcast(I32))
         nc.sync.dma_start(idx[:], offs)
         load_w1(0)
         nc.sync.dma_start(tab_w[0][:], tab_words[0].rearrange("p t i -> p (t i)").bitcast(I32))
         nc.sync.dma_start(w4_raw[:].bitcast(I32), w4_words[0].bitcast(I32))
         for q in range(4):
-            nc.sync.dma_start(tab_s[32 * q : 32 * q + 8, :].bitcast(I32), tab_scales[:, 4 * q : 4 * q + 4, :].bitcast(I32))
-        nc.sync.dma_start(tab_w[1][:], tab_words[1].rearrange("p t i -> p (t i)").bitcast(I32))
-        for q in range(4):
             nc.sync.dma_start(w4s_raw[32 * q : 32 * q + 4, :].bitcast(I32), w4_scales[0, 4 * q : 4 * q + 4, :].bitcast(I32))
+        nc.sync.dma_start(tab_w[1][:], tab_words[1].rearrange("p t i -> p (t i)").bitcast(I32))
+        nc.sync.dma_start(idx2[:], offs2)
         for q in range(4):
             nc.sync.dma_start(wgs_sb[32 * q : 32 * (q + 1)], wgs.rearrange("(p t) c -> p t c", t=4))
-        nc.sync.dma_start(idx2[:], offs2)
         load_lot_page(0)
         nc.sync.dma_start(idx3[:], offs3)
         load_clean(0)
@@ -89,7 +89,7 @@ def tile_list_cork_taint_deviation_kernel(
         for k in range(2, TILES):
             load_lot_page(k)
             load_clean(k)
-            if k == 4:
+            if k == 3:
                 load_w1(2)
         with nc.allow_non_contiguous_dma(reason="one offset a partition"):
             nc.sync.dma_start(slot_sb[:], slotv.rearrange("(m p) -> p m", p=P))
@@ -133,13 +133,16 @@ def tile_list_cork_taint_deviation_kernel(
             )
 
         def chain(k):
-            shrink[k] = ring.tile([P, S], F32, name="shrink", bufs=AHEAD + 2)
+            shrink[k] = ring.tile([P, S], F32, name="shrink", bufs=AHEAD + 3)
             nc.scalar.activation(shrink[k][:], a_ps[k][:], ACT.Abs)
             nc.scalar.activation(shrink[k][:], shrink[k][:], ACT.Abs_reciprocal_sqrt, bias=1.0)
             nc.scalar.activation(shrink[k][:], shrink[k][:], ACT.Square)
 
         def weigh(k):
-            nc.vector.tensor_tensor(lot_sb[k][:], lot_sb[k][:], wgs_sb[:, k % 4, :], ALU.mult)
+            engine = nc.vector if k == 0 else nc.gpsimd
+            engine.tensor_tensor(lot_sb[k][:], lot_sb[k][:], wgs_sb[:, k % 4, :], ALU.mult)
+            if k > 0:
+                nc.gpsimd.tensor_tensor(lot_sb[k][:], lot_sb[k][:], shrink[k][:], ALU.mult)
 
         woven0 = weave_w1(0, nc.vector.tensor_copy)
         deal_w4_words(0)
@@ -154,9 +157,10 @@ def tile_list_cork_taint_deviation_kernel(
             readout(k)
         deal_w4_scales(1)
         deal_w4_scales(2)
-        for k in range(AHEAD):
+        for k in range(4):
             chain(k)
         weigh(0)
+        weigh(1)
 
         page_c = [[keep.tile([P, 512], U32, name="page_c%d%d" % (b, h), align_bytes=64) for h in range(2)] for b in range(PASSES)]
         page_s = [[keep.tile([P, 512], U8, name="page_s%d%d" % (b, h), align_bytes=64) for h in range(2)] for b in range(PASSES)]
@@ -165,10 +169,7 @@ def tile_list_cork_taint_deviation_kernel(
         e_ps = {}
 
         def weave(dst, src, slots):
-            nc.scalar.copy(
-                dst[:].rearrange("p (c i) t -> p c t i", i=4)[:, :, 0:slots, :],
-                src.rearrange("p t (c i) -> p c t i", i=4)[:, :, 0:slots, :],
-            )
+            nc.scalar.copy(dst[:, :, 0:slots], src.rearrange("p t c -> p c t")[:, :, 0:slots])
 
         def scores(b, page_woven, x_woven):
             for h in range(2):
@@ -185,59 +186,78 @@ def tile_list_cork_taint_deviation_kernel(
                     rhs=x_c[b][:].bitcast(FP8X4), rhs_scale=x_s[b][:], start=(b == 0), stop=(b == PASSES - 1),
                 )
 
-        pending = []
-        for k in range(TILES):
+        shifted, page_bf, x_bf, page_woven, x_woven = {}, {}, {}, {}, {}
+
+        def put_and_pick(k):
             b, t = divmod(k, 4)
-            last = b == PASSES - 1
             if t == 0:
-                page_bf = ring.tile([P, 4, T2], BF16, name="page_bf")
-                x_bf = ring.tile([P, 4, NP], BF16, name="x_bf")
-                page_woven = [ring.tile([P, 512, 4], BF16, name="page_woven%d" % (h), align_bytes=64) for h in range(2)]
-                x_woven = ring.tile([P, NP, 4], BF16, name="x_woven", align_bytes=64)
-            if t == 0 and not last:
-                quant_w1(b + 1, weave_w1(b + 1, nc.scalar.copy))
-                for kk in range(4 * b + 4, 4 * b + 8):
-                    readout(kk)
-            nc.vector.tensor_tensor(page_sb[k][:].indirect(idx2[:]), shrink[k][:], lot_sb[k][:], ALU.mult)
-            if k + 1 < TILES:
-                weigh(k + 1)
-            shifted = ring.tile([P, NP], F32, name="shifted")
-            nc.vector.tensor_tensor(shifted[:], page_sb[k][:].indirect(idx3[:]), clean_sb[k][:], ALU.add)
+                page_bf[b] = ring.tile([P, 4, T2], BF16, name="page_bf")
+                x_bf[b] = ring.tile([P, 4, NP], BF16, name="x_bf")
+                page_woven[b] = [ring.tile([P, 512, 4], BF16, name="page_woven%d" % h, align_bytes=64) for h in range(2)]
+                x_woven[b] = ring.tile([P, NP, 4], BF16, name="x_woven", align_bytes=64)
+            if k == 0:
+                nc.vector.tensor_tensor(page_sb[k][:].indirect(idx2[:]), shrink[k][:], lot_sb[k][:], ALU.mult)
+            else:
+                nc.vector.tensor_copy(page_sb[k][:].indirect(idx2[:]), lot_sb[k][:])
+            shifted[k] = ring.tile([P, NP], F32, name="shifted", bufs=3)
+            if k == TILES - 1:
+                nc.vector.tensor_tensor(shifted[k][:], page_sb[k][:].indirect(idx3[:]), clean_sb[k][:], ALU.add)
+            else:
+                nc.vector.tensor_copy(shifted[k][:], page_sb[k][:].indirect(idx3[:]))
+            if k >= TILES - 2:
+                nc.vector.tensor_copy(page_woven[b][1][:, :, t], page_sb[k][:, 512:1024])
+
+        def round_rows(k):
+            b, t = divmod(k, 4)
+            gain = gv_sb[:, b, t : t + 1]
+            if k < TILES - 1:
+                summed = shrink[min(k + 2, TILES - 1)] if k < TILES - 2 else shifted[k]
+                nc.gpsimd.tensor_tensor(summed[:], shifted[k][:], clean_sb[k][:], ALU.add)
+            else:
+                summed = shifted[k]
+            if k < TILES - 2:
+                nc.scalar.copy(page_bf[b][:, t, :], page_sb[k][:])
+            elif k == TILES - 2:
+                nc.scalar.copy(page_bf[b][:, t, 0:512], page_sb[k][:, 0:512])
+            else:
+                nc.scalar.copy(page_woven[b][0][:, :, t], page_sb[k][:, 0:512])
+            if k < TILES - 1:
+                nc.scalar.activation(x_bf[b][:, t, :], summed[:], ACT.Copy, scale=gain)
+            else:
+                nc.scalar.activation(x_woven[b][:, :, t], summed[:], ACT.Copy, scale=gain)
+
+        def weave_page(b, h, slots):
+            weave(page_woven[b][h], page_bf[b][:, :, 512 * h : 512 * (h + 1)], slots)
+
+        def prepare_pass(b):
+            quant_w1(b, weave_w1(b, nc.scalar.copy))
+            for k in range(4 * b, 4 * b + 4):
+                readout(k)
+
+        prepare_pass(1)
+        chain(4)
+        for k in range(TILES):
+            put_and_pick(k)
+            if k + 2 < TILES:
+                weigh(k + 2)
+            if k + AHEAD == 8:
+                prepare_pass(2)
             if k + AHEAD < TILES:
                 chain(k + AHEAD)
-            gain = gv_sb[:, b, t : t + 1]
-            if not last:
-                nc.scalar.copy(page_bf[:, t, :], page_sb[k][:])
-                nc.scalar.activation(x_bf[:, t, :], shifted[:], ACT.Copy, scale=gain)
-                if t == 3:
-                    for h in range(2):
-                        weave(page_woven[h], page_bf[:, :, 512 * h : 512 * (h + 1)], 4)
-                    weave(x_woven, x_bf[:], 4)
-                    pending.append((b, page_woven, x_woven))
-            else:
-                if t < 2:
-                    nc.scalar.copy(page_bf[:, t, :], page_sb[k][:])
-                elif t == 2:
-                    nc.scalar.copy(page_bf[:, t, 0:512], page_sb[k][:, 0:512])
-                else:
-                    nc.scalar.copy(page_woven[0][:, :, t], page_sb[k][:, 0:512])
-                if t >= 2:
-                    nc.vector.tensor_copy(page_woven[1][:, :, t], page_sb[k][:, 512:1024])
-                if t == 1:
-                    weave(page_woven[1], page_bf[:, :, 512:1024], 2)
-                if t < 3:
-                    nc.scalar.activation(x_bf[:, t, :], shifted[:], ACT.Copy, scale=gain)
-                else:
-                    nc.scalar.activation(x_woven[:, :, t], shifted[:], ACT.Copy, scale=gain)
-                if t == 2:
-                    weave(page_woven[0], page_bf[:, :, 0:512], 3)
-                    weave(x_woven, x_bf[:], 3)
-                if t == 3:
-                    pending.append((b, page_woven, x_woven))
-            if pending and (t == 0 or k == TILES - 1):
-                for item in pending:
-                    scores(*item)
-                pending.clear()
+            if k > 0:
+                round_rows(k - 1)
+            b, t = divmod(k, 4)
+            if b > 0 and t < 2:
+                weave_page(b - 1, t, 4)
+            if b > 0 and t == 2:
+                weave(x_woven[b - 1], x_bf[b - 1][:], 4)
+                scores(b - 1, page_woven[b - 1], x_woven[b - 1])
+            if k == TILES - 2:
+                weave_page(b, 1, 2)
+        weave_page(2, 0, 3)
+        weave(x_woven[2], x_bf[2][:], 3)
+        round_rows(TILES - 1)
+        scores(2, page_woven[2], x_woven[2])
 
         for m in range(T2 // P):
             staged = ring.tile([P, NP], F32, name="staged", bufs=4)

@@ -18,7 +18,6 @@ P = 128
 PASSES = H // 512
 TILES = H // P
 FLOPS = 2 * K * H * S + 2 * H * T2 * NP
-AHEAD = 5
 
 
 def tile_list_cork_taint_deviation_kernel(
@@ -58,7 +57,10 @@ def tile_list_cork_taint_deviation_kernel(
             return src.rearrange("(b p t) c -> b t p c", p=P, t=4)[k // 4, k % 4]
 
         def load_lot_page(k):
-            lot_sb[k] = ring.tile([P, S], F32, name="lot_sb", bufs=6)
+            if k == TILES - 1:
+                lot_sb[k] = keep.tile([P, S], F32, name="lot_last", tag="after_last_scatter", align_bytes=64)
+            else:
+                lot_sb[k] = ring.tile([P, S], F32, name="lot_sb", bufs=6)
             nc.sync.dma_start(lot_sb[k][:], rows(lotw, k))
             page_sb[k] = ring.tile([P, T2], F32, name="page_sb", bufs=8)
             nc.sync.dma_start(page_sb[k][:], rows(page0, k))
@@ -67,15 +69,15 @@ def tile_list_cork_taint_deviation_kernel(
             clean_sb[k] = ring.tile([P, NP], F32, name="clean_sb", bufs=6)
             nc.sync.dma_start(clean_sb[k][:], rows(cleanm, k))
 
-        for q in range(4):
-            nc.gpsimd.dma_start(tab_s[32 * q : 32 * q + 8, :].bitcast(I32), tab_scales[:, 4 * q : 4 * q + 4, :].bitcast(I32))
         nc.sync.dma_start(idx[:], offs)
         load_w1(0)
         nc.sync.dma_start(tab_w[0][:], tab_words[0].rearrange("p t i -> p (t i)").bitcast(I32))
+        for q in range(4):
+            nc.sync.dma_start(tab_s[32 * q : 32 * q + 8, :].bitcast(I32), tab_scales[:, 4 * q : 4 * q + 4, :].bitcast(I32))
         nc.sync.dma_start(w4_raw[:].bitcast(I32), w4_words[0].bitcast(I32))
+        nc.sync.dma_start(tab_w[1][:], tab_words[1].rearrange("p t i -> p (t i)").bitcast(I32))
         for q in range(4):
             nc.sync.dma_start(w4s_raw[32 * q : 32 * q + 4, :].bitcast(I32), w4_scales[0, 4 * q : 4 * q + 4, :].bitcast(I32))
-        nc.sync.dma_start(tab_w[1][:], tab_words[1].rearrange("p t i -> p (t i)").bitcast(I32))
         nc.sync.dma_start(idx2[:], offs2)
         for q in range(4):
             nc.sync.dma_start(wgs_sb[32 * q : 32 * (q + 1)], wgs.rearrange("(p t) c -> p t c", t=4))
@@ -96,7 +98,7 @@ def tile_list_cork_taint_deviation_kernel(
 
         w4_c = [keep.tile([P, 4, P, 2], U8, name="w4_c%d" % (b), align_bytes=64) for b in range(PASSES)]
         w4_s = [keep.tile([P, 4, P], U8, name="w4_s%d" % (b), align_bytes=64) for b in range(PASSES)]
-        w1_c = [keep.tile([P, 512], U32, name="w1_c%d" % (b), align_bytes=64) for b in range(PASSES)]
+        w1_c, w1_woven = {}, {}
         w1_s = [keep.tile([P, 512], U8, name="w1_s%d" % (b), align_bytes=64) for b in range(PASSES)]
         v_c = [keep.tile([P, S], U32, name="v_c%d" % (a), align_bytes=64) for a in range(2)]
         v_s = keep.tile([P, S], U8, name="v_s", align_bytes=64)
@@ -110,12 +112,12 @@ def tile_list_cork_taint_deviation_kernel(
             nc.vector.tensor_copy(w4_s[b][:], w4s_raw[:, 512 * b : 512 * (b + 1)].rearrange("p (m t) -> p t m", t=4))
 
         def weave_w1(b, copy):
-            woven = ring.tile([P, 4, P, 4], BF16, name="w1_woven", align_bytes=64)
-            copy(woven[:].rearrange("p t m j -> p m j t"), w1_raw[b][:].rearrange("p j (m t) -> p m j t", t=4))
-            return woven
+            w1_woven[b] = ring.tile([P, 4, P, 4], BF16, name="w1_woven", align_bytes=64)
+            copy(w1_woven[b][:].rearrange("p t m j -> p m t j"), w1_raw[b][:].rearrange("p j (m t) -> p m t j", t=4))
 
-        def quant_w1(b, woven):
-            nc.vector.quantize_mx(w1_c[b][:].bitcast(FP8X4), w1_s[b][:], woven[:].rearrange("p t m j -> p (t m j)"))
+        def quant_w1(b):
+            w1_c[b] = keep.tile([P, 512], U32, name="w1_c%d" % b, align_bytes=64)
+            nc.vector.quantize_mx(w1_c[b][:].bitcast(FP8X4), w1_s[b][:], w1_woven[b][:].rearrange("p t m j -> p (t m j)"))
 
         a_ps, shrink = {}, {}
 
@@ -133,133 +135,150 @@ def tile_list_cork_taint_deviation_kernel(
             )
 
         def chain(k):
-            shrink[k] = ring.tile([P, S], F32, name="shrink", bufs=AHEAD + 3)
-            nc.scalar.activation(shrink[k][:], a_ps[k][:], ACT.Abs)
-            nc.scalar.activation(shrink[k][:], shrink[k][:], ACT.Abs_reciprocal_sqrt, bias=1.0)
-            nc.scalar.activation(shrink[k][:], shrink[k][:], ACT.Square)
+            pair = ring.tile([P, 2, S], F32, name="pair", bufs=3)
+            for u in range(2):
+                shrink[k + u] = pair[:, u, :]
+                nc.scalar.activation(shrink[k + u], a_ps[k + u][:], ACT.Abs)
+            parts = [shrink[0][:, 0:256], shrink[0][:, 256:512], shrink[1]] if k == 0 else [pair[:]]
+            for part in parts:
+                nc.scalar.activation(part, part, ACT.Abs_reciprocal_sqrt, bias=1.0)
+                nc.scalar.activation(part, part, ACT.Square)
 
         def weigh(k):
-            engine = nc.vector if k == 0 else nc.gpsimd
-            engine.tensor_tensor(lot_sb[k][:], lot_sb[k][:], wgs_sb[:, k % 4, :], ALU.mult)
-            if k > 0:
-                nc.gpsimd.tensor_tensor(lot_sb[k][:], lot_sb[k][:], shrink[k][:], ALU.mult)
+            nc.vector.tensor_tensor(lot_sb[k][:], lot_sb[k][:], wgs_sb[:, k % 4, :], ALU.mult)
 
-        woven0 = weave_w1(0, nc.vector.tensor_copy)
+        weave_w1(0, nc.vector.tensor_copy)
         deal_w4_words(0)
-        quant_w1(0, woven0)
+        quant_w1(0)
         nc.vector.tensor_copy(v_c[0][:], tab_w[0][:].bitcast(U32).indirect(idx[:]))
         nc.vector.tensor_copy(v_s[:], tab_s[:].indirect(idx[:]))
-        deal_w4_words(1)
-        deal_w4_words(2)
-        deal_w4_scales(0)
         nc.vector.tensor_copy(v_c[1][:], tab_w[1][:].bitcast(U32).indirect(idx[:]))
+        deal_w4_scales(0)
         for k in range(4):
             readout(k)
+        deal_w4_words(1)
+        deal_w4_words(2)
         deal_w4_scales(1)
         deal_w4_scales(2)
-        for k in range(4):
-            chain(k)
+        chain(0)
+        chain(2)
         weigh(0)
-        weigh(1)
 
-        page_c = [[keep.tile([P, 512], U32, name="page_c%d%d" % (b, h), align_bytes=64) for h in range(2)] for b in range(PASSES)]
-        page_s = [[keep.tile([P, 512], U8, name="page_s%d%d" % (b, h), align_bytes=64) for h in range(2)] for b in range(PASSES)]
-        x_c = [keep.tile([P, NP], U32, name="x_c%d" % (b), align_bytes=64) for b in range(PASSES)]
-        x_s = [keep.tile([P, NP], U8, name="x_s%d" % (b), align_bytes=64) for b in range(PASSES)]
-        e_ps = {}
+        page_c = [keep.tile([P, T2], U32, name="page_c%d" % b, align_bytes=64) for b in range(PASSES)]
+        page_s = [keep.tile([P, T2], U8, name="page_s%d" % b, align_bytes=64) for b in range(PASSES)]
+        x_s = [keep.tile([P, NP], U8, name="x_s%d" % b, align_bytes=64) for b in range(PASSES)]
+        x_c, e_ps, shifted, page_bf, x_bf, page_woven, x_woven = {}, {}, {}, {}, {}, {}, {}
 
         def weave(dst, src, slots):
             nc.scalar.copy(dst[:, :, 0:slots], src.rearrange("p t c -> p c t")[:, :, 0:slots])
 
-        def scores(b, page_woven, x_woven):
-            for h in range(2):
+        def weave_x(b, slots):
+            x_woven[b] = ring.tile([P, NP, 4], BF16, name="x_woven", align_bytes=64, bufs=3)
+            weave(x_woven[b][:], x_bf[b][:], slots)
+
+        def weave_page(b, h, slots):
+            if h == 0:
+                page_woven[b] = ring.tile([P, T2, 4], BF16, name="page_woven", align_bytes=64)
+            cols = slice(512 * h, 512 * (h + 1))
+            weave(page_woven[b][:, cols, :], page_bf[b][:, :, cols], slots)
+
+        def quant_page(b, pieces):
+            for h in range(pieces):
+                cols = slice(T2 // pieces * h, T2 // pieces * (h + 1))
                 nc.vector.quantize_mx(
-                    page_c[b][h][:].bitcast(FP8X4), page_s[b][h][:], page_woven[h][:].rearrange("p c t -> p (c t)")
+                    page_c[b][:, cols].bitcast(FP8X4), page_s[b][:, cols], page_woven[b][:, cols, :].rearrange("p c t -> p (c t)")
                 )
-            nc.vector.quantize_mx(x_c[b][:].bitcast(FP8X4), x_s[b][:], x_woven[:].rearrange("p c t -> p (c t)"))
+
+        def quant_x(b):
+            tag = "after_last_scatter" if b == 1 else "x_c%d" % b
+            x_c[b] = keep.tile([P, NP], U32, name="x_c", tag=tag, align_bytes=64)
+            nc.vector.quantize_mx(x_c[b][:].bitcast(FP8X4), x_s[b][:], x_woven[b][:].rearrange("p c t -> p (c t)"))
+
+        def scores(b):
             for m in range(T2 // P):
                 if b == 0:
-                    e_ps[m] = psum.tile([P, NP], F32, name="bank%d" % (m))
-                cols = slice(P * (m % 4), P * (m % 4 + 1))
+                    e_ps[m] = psum.tile([P, NP], F32, name="bank%d" % m)
+                cols = slice(P * m, P * (m + 1))
                 nc.tensor.matmul_mx(
-                    e_ps[m][:], lhsT=page_c[b][m // 4][:, cols].bitcast(FP8X4), lhsT_scale=page_s[b][m // 4][:, cols],
+                    e_ps[m][:], lhsT=page_c[b][:, cols].bitcast(FP8X4), lhsT_scale=page_s[b][:, cols],
                     rhs=x_c[b][:].bitcast(FP8X4), rhs_scale=x_s[b][:], start=(b == 0), stop=(b == PASSES - 1),
                 )
 
-        shifted, page_bf, x_bf, page_woven, x_woven = {}, {}, {}, {}, {}
+        def put(k):
+            pieces = 2 if k == 0 else 1
+            for h in range(pieces):
+                cols = slice(S // pieces * h, S // pieces * (h + 1))
+                offsets = idx2[:, cols.start // 16 : cols.stop // 16]
+                nc.vector.tensor_tensor(page_sb[k][:].indirect(offsets), shrink[k][:, cols], lot_sb[k][:, cols], ALU.mult)
 
-        def put_and_pick(k):
+        def pick(k):
+            b, t = divmod(k, 4)
+            shifted[k] = ring.tile([P, NP], F32, name="shifted", bufs=3)
+            nc.vector.tensor_tensor(shifted[k][:], page_sb[k][:].indirect(idx3[:]), clean_sb[k][:], ALU.add)
+            if k >= TILES - 2:
+                nc.vector.tensor_scalar(x_woven[b][:, :, t], shifted[k][:], gv_sb[:, b, t : t + 1], None, ALU.mult)
+
+        def round_page(k):
             b, t = divmod(k, 4)
             if t == 0:
                 page_bf[b] = ring.tile([P, 4, T2], BF16, name="page_bf")
-                x_bf[b] = ring.tile([P, 4, NP], BF16, name="x_bf")
-                page_woven[b] = [ring.tile([P, 512, 4], BF16, name="page_woven%d" % h, align_bytes=64) for h in range(2)]
-                x_woven[b] = ring.tile([P, NP, 4], BF16, name="x_woven", align_bytes=64)
-            if k == 0:
-                nc.vector.tensor_tensor(page_sb[k][:].indirect(idx2[:]), shrink[k][:], lot_sb[k][:], ALU.mult)
-            else:
-                nc.vector.tensor_copy(page_sb[k][:].indirect(idx2[:]), lot_sb[k][:])
-            shifted[k] = ring.tile([P, NP], F32, name="shifted", bufs=3)
-            if k == TILES - 1:
-                nc.vector.tensor_tensor(shifted[k][:], page_sb[k][:].indirect(idx3[:]), clean_sb[k][:], ALU.add)
-            else:
-                nc.vector.tensor_copy(shifted[k][:], page_sb[k][:].indirect(idx3[:]))
-            if k >= TILES - 2:
-                nc.vector.tensor_copy(page_woven[b][1][:, :, t], page_sb[k][:, 512:1024])
-
-        def round_rows(k):
-            b, t = divmod(k, 4)
-            gain = gv_sb[:, b, t : t + 1]
             if k < TILES - 1:
-                summed = shrink[min(k + 2, TILES - 1)] if k < TILES - 2 else shifted[k]
-                nc.gpsimd.tensor_tensor(summed[:], shifted[k][:], clean_sb[k][:], ALU.add)
-            else:
-                summed = shifted[k]
-            if k < TILES - 2:
                 nc.scalar.copy(page_bf[b][:, t, :], page_sb[k][:])
-            elif k == TILES - 2:
-                nc.scalar.copy(page_bf[b][:, t, 0:512], page_sb[k][:, 0:512])
             else:
-                nc.scalar.copy(page_woven[b][0][:, :, t], page_sb[k][:, 0:512])
-            if k < TILES - 1:
-                nc.scalar.activation(x_bf[b][:, t, :], summed[:], ACT.Copy, scale=gain)
-            else:
-                nc.scalar.activation(x_woven[b][:, :, t], summed[:], ACT.Copy, scale=gain)
+                for h in range(2):
+                    cols = slice(512 * h, 512 * (h + 1))
+                    nc.scalar.copy(page_woven[b][:, cols, t], page_sb[k][:, cols])
 
-        def weave_page(b, h, slots):
-            weave(page_woven[b][h], page_bf[b][:, :, 512 * h : 512 * (h + 1)], slots)
-
-        def prepare_pass(b):
-            quant_w1(b, weave_w1(b, nc.scalar.copy))
-            for k in range(4 * b, 4 * b + 4):
-                readout(k)
-
-        prepare_pass(1)
-        chain(4)
-        for k in range(TILES):
-            put_and_pick(k)
-            if k + 2 < TILES:
-                weigh(k + 2)
-            if k + AHEAD == 8:
-                prepare_pass(2)
-            if k + AHEAD < TILES:
-                chain(k + AHEAD)
-            if k > 0:
-                round_rows(k - 1)
+        def round_x(k):
             b, t = divmod(k, 4)
-            if b > 0 and t < 2:
-                weave_page(b - 1, t, 4)
-            if b > 0 and t == 2:
-                weave(x_woven[b - 1], x_bf[b - 1][:], 4)
-                scores(b - 1, page_woven[b - 1], x_woven[b - 1])
+            if t == 0:
+                x_bf[b] = ring.tile([P, 4, NP], BF16, name="x_bf")
+            nc.scalar.activation(x_bf[b][:, t, :], shifted[k][:], ACT.Copy, scale=gv_sb[:, b, t : t + 1])
+
+        for k in range(TILES):
+            b, t = divmod(k, 4)
+            if t == 0 and b + 1 < PASSES:
+                weave_w1(b + 1, nc.scalar.copy)
+                quant_w1(b + 1)
+                for tile in range(4 * b + 4, 4 * b + 8):
+                    readout(tile)
+            put(k)
+            if k + 1 < TILES:
+                weigh(k + 1)
+            else:
+                quant_x(1)
+                scores(1)
             if k == TILES - 2:
-                weave_page(b, 1, 2)
-        weave_page(2, 0, 3)
-        weave(x_woven[2], x_bf[2][:], 3)
-        round_rows(TILES - 1)
-        scores(2, page_woven[2], x_woven[2])
+                weave_x(b, 2)
+            pick(k)
+            if k % 2 == 1 and k + 3 < TILES:
+                chain(k + 3)
+            if k < TILES - 1:
+                round_page(k)
+            if k < TILES - 2:
+                round_x(k)
+            if b > 0 and t == 0:
+                for h in range(2):
+                    weave_page(b - 1, h, 4)
+            if b > 0 and t == 1:
+                weave_x(b - 1, 4)
+                quant_page(b - 1, 1)
+            if k == 5:
+                quant_x(0)
+                scores(0)
+            if k == TILES - 2:
+                for h in range(2):
+                    weave_page(b, h, 3)
+        round_page(TILES - 1)
+        quant_x(2)
+        quant_page(2, 2)
+        scores(2)
 
         for m in range(T2 // P):
-            staged = ring.tile([P, NP], F32, name="staged", bufs=4)
-            nc.scalar.activation(staged[:], e_ps[m][:], ACT.Abs, bias=slot_sb[:, m : m + 1], scale=-1.0)
+            staged = ring.tile([P, NP], F32, name="staged", bufs=5)
+            if m in (2, 5):
+                nc.vector.tensor_scalar(staged[:], e_ps[m][:], slot_sb[:, m : m + 1], -1.0, ALU.subtract, ALU.mult)
+                nc.vector.scalar_tensor_tensor(staged[:], staged[:], -1.0, staged[:], ALU.mult, ALU.max)
+            else:
+                nc.scalar.activation(staged[:], e_ps[m][:], ACT.Abs, bias=slot_sb[:, m : m + 1], scale=-1.0)
             nc.sync.dma_start(out[P * m : P * (m + 1), :], staged[:])

from contextlib import ExitStack

import concourse.mybir as mybir

F32 = mybir.dt.float32
BF16 = mybir.dt.bfloat16
I32 = mybir.dt.int32
U32 = mybir.dt.uint32
U16 = mybir.dt.uint16
U8 = mybir.dt.uint8
FP8X4 = mybir.dt.float8_e4m3fn_x4
FP4X4 = mybir.dt.float4_e2m1fn_x4
ACT = mybir.ActivationFunctionType
ALU = mybir.AluOpType

K, KA, T, S, H, T2, NP = 1024, 512, 2048, 512, 1536, 1024, 512
P = 128
PASSES = H // 512
TILES = H // P
FLOPS = 2 * K * H * S + 2 * H * T2 * NP


def tile_list_cork_taint_deviation_kernel(
    tc, tab_words, tab_scales, offs, offs2, offs3, w4_words, w4_scales, w1, lotw, wgs, page0, cleanm, gv, slotv, out
):
    nc = tc.nc
    with ExitStack() as ctx:
        keep = ctx.enter_context(tc.tile_pool(name="keep", bufs=1))
        ring = ctx.enter_context(tc.tile_pool(name="ring", bufs=2))
        psum = ctx.enter_context(tc.psum_pool(name="psum", bufs=1))

        idx = keep.tile([P, S // 16], U16, name="idx")
        idx2 = keep.tile([P, S // 16], U16, name="idx2")
        idx3 = keep.tile([P, NP // 16], U16, name="idx3")
        tab_w = [keep.tile([P, T], I32, name="tab_w%d" % (a)) for a in range(2)]
        tab_s = keep.tile([P, T], U8, name="tab_s")
        w4_raw = keep.tile([P, 2 * H], U8, name="w4_raw")
        w4s_raw = keep.tile([P, H], U8, name="w4s_raw")
        wgs_sb = keep.tile([P, 4, S], F32, name="wgs_sb")
        gv_sb = keep.tile([P, PASSES, 4], F32, name="gv_sb")
        slot_sb = keep.tile([P, T2 // P], F32, name="slot_sb")
        warm = keep.tile([P, 1], F32, name="warm")
        warm2 = keep.tile([P, 1], F32, name="warm2")

        nc.gpsimd.memset(tab_s[:].bitcast(I32), 0)
        nc.vector.memset(w4s_raw[:].bitcast(I32), 0)
        nc.vector.memset(warm[:], 1.0)
        nc.scalar.activation(warm2[:], warm[:], ACT.Abs_reciprocal_sqrt)

        w1_raw, lot_sb, page_sb, clean_sb = {}, {}, {}, {}

        def load_w1(b):
            w1_raw[b] = ring.tile([P, 4, 512], F32, name="w1_raw", bufs=2)
            nc.sync.dma_start(w1_raw[b][:], w1.rearrange("(p j) r -> p j r", j=4)[:, :, 512 * b : 512 * (b + 1)])

        def rows(src, k):
            return src.rearrange("(b p t) c -> b t p c", p=P, t=4)[k // 4, k % 4]

        def load_lot_page(k):
            if k == TILES - 1:
                lot_sb[k] = keep.tile([P, S], F32, name="lot_last", tag="after_last_scatter", align_bytes=64)
            else:
                lot_sb[k] = ring.tile([P, S], F32, name="lot_sb", bufs=6)
            nc.sync.dma_start(lot_sb[k][:], rows(lotw, k))
            page_sb[k] = ring.tile([P, T2], F32, name="page_sb", bufs=8)
            nc.sync.dma_start(page_sb[k][:], rows(page0, k))

        def load_clean(k):
            clean_sb[k] = ring.tile([P, NP], F32, name="clean_sb", bufs=6)
            nc.sync.dma_start(clean_sb[k][:], rows(cleanm, k))

        nc.sync.dma_start(idx[:], offs)
        load_w1(0)
        nc.sync.dma_start(tab_w[0][:], tab_words[0].rearrange("p t i -> p (t i)").bitcast(I32))
        for q in range(4):
            nc.sync.dma_start(tab_s[32 * q : 32 * q + 8, :].bitcast(I32), tab_scales[:, 4 * q : 4 * q + 4, :].bitcast(I32))
        nc.sync.dma_start(w4_raw[:].bitcast(I32), w4_words[0].bitcast(I32))
        nc.sync.dma_start(tab_w[1][:], tab_words[1].rearrange("p t i -> p (t i)").bitcast(I32))
        for q in range(4):
            nc.sync.dma_start(w4s_raw[32 * q : 32 * q + 4, :].bitcast(I32), w4_scales[0, 4 * q : 4 * q + 4, :].bitcast(I32))
        nc.sync.dma_start(idx2[:], offs2)
        for q in range(4):
            nc.sync.dma_start(wgs_sb[32 * q : 32 * (q + 1)], wgs.rearrange("(p t) c -> p t c", t=4))
        load_lot_page(0)
        nc.sync.dma_start(idx3[:], offs3)
        load_clean(0)
        nc.sync.dma_start(gv_sb[:], gv.rearrange("(b p t) -> p b t", p=P, t=4))
        load_lot_page(1)
        load_clean(1)
        load_w1(1)
        for k in range(2, TILES):
            load_lot_page(k)
            load_clean(k)
            if k == 3:
                load_w1(2)
        with nc.allow_non_contiguous_dma(reason="one offset a partition"):
            nc.sync.dma_start(slot_sb[:], slotv.rearrange("(m p) -> p m", p=P))

        w4_c = [keep.tile([P, 4, P, 2], U8, name="w4_c%d" % (b), align_bytes=64) for b in range(PASSES)]
        w4_s = [keep.tile([P, 4, P], U8, name="w4_s%d" % (b), align_bytes=64) for b in range(PASSES)]
        w1_c, w1_woven = {}, {}
        w1_s = [keep.tile([P, 512], U8, name="w1_s%d" % (b), align_bytes=64) for b in range(PASSES)]
        v_c = [keep.tile([P, S], U32, name="v_c%d" % (a), align_bytes=64) for a in range(2)]
        v_s = keep.tile([P, S], U8, name="v_s", align_bytes=64)

        def deal_w4_words(b):
            nc.vector.tensor_copy(
                w4_c[b][:], w4_raw[:, 1024 * b : 1024 * (b + 1)].rearrange("p (m t e) -> p t m e", t=4, e=2)
            )

        def deal_w4_scales(b):
            nc.vector.tensor_copy(w4_s[b][:], w4s_raw[:, 512 * b : 512 * (b + 1)].rearrange("p (m t) -> p t m", t=4))

        def weave_w1(b, copy):
            w1_woven[b] = ring.tile([P, 4, P, 4], BF16, name="w1_woven", align_bytes=64)
            copy(w1_woven[b][:].rearrange("p t m j -> p m t j"), w1_raw[b][:].rearrange("p j (m t) -> p m t j", t=4))

        def quant_w1(b):
            w1_c[b] = keep.tile([P, 512], U32, name="w1_c%d" % b, align_bytes=64)
            nc.vector.quantize_mx(w1_c[b][:].bitcast(FP8X4), w1_s[b][:], w1_woven[b][:].rearrange("p t m j -> p (t m j)"))

        a_ps, shrink = {}, {}

        def readout(k):
            b, t = divmod(k, 4)
            a_ps[k] = psum.tile([P, S], F32, name="bank%d" % (k % 8))
            cols = slice(P * t, P * (t + 1))
            nc.tensor.matmul_mx(
                a_ps[k][:], lhsT=w4_c[b][:, t].rearrange("p m e -> p (m e)").bitcast(FP4X4), lhsT_scale=w4_s[b][:, t],
                rhs=v_c[0][:].bitcast(FP8X4), rhs_scale=v_s[:], start=True, stop=False,
            )
            nc.tensor.matmul_mx(
                a_ps[k][:], lhsT=w1_c[b][:, cols].bitcast(FP8X4), lhsT_scale=w1_s[b][:, cols],
                rhs=v_c[1][:].bitcast(FP8X4), rhs_scale=v_s[4:P, :], start=False, stop=True,
            )

        def chain(k):
            pair = ring.tile([P, 2, S], F32, name="pair", bufs=3)
            for u in range(2):
                shrink[k + u] = pair[:, u, :]
                nc.scalar.activation(shrink[k + u], a_ps[k + u][:], ACT.Abs)
            parts = [shrink[0][:, 0:256], shrink[0][:, 256:512], shrink[1]] if k == 0 else [pair[:]]
            for part in parts:
                nc.scalar.activation(part, part, ACT.Abs_reciprocal_sqrt, bias=1.0)
                nc.scalar.activation(part, part, ACT.Square)

        def weigh(k):
            nc.vector.tensor_tensor(lot_sb[k][:], lot_sb[k][:], wgs_sb[:, k % 4, :], ALU.mult)

        weave_w1(0, nc.vector.tensor_copy)
        deal_w4_words(0)
        quant_w1(0)
        nc.vector.tensor_copy(v_c[0][:], tab_w[0][:].bitcast(U32).indirect(idx[:]))
        nc.vector.tensor_copy(v_s[:], tab_s[:].indirect(idx[:]))
        nc.vector.tensor_copy(v_c[1][:], tab_w[1][:].bitcast(U32).indirect(idx[:]))
        deal_w4_scales(0)
        for k in range(4):
            readout(k)
        deal_w4_words(1)
        deal_w4_words(2)
        deal_w4_scales(1)
        deal_w4_scales(2)
        chain(0)
        chain(2)
        weigh(0)

        page_c = [keep.tile([P, T2], U32, name="page_c%d" % b, align_bytes=64) for b in range(PASSES)]
        page_s = [keep.tile([P, T2], U8, name="page_s%d" % b, align_bytes=64) for b in range(PASSES)]
        x_s = [keep.tile([P, NP], U8, name="x_s%d" % b, align_bytes=64) for b in range(PASSES)]
        x_c, e_ps, shifted, page_bf, x_bf, page_woven, x_woven = {}, {}, {}, {}, {}, {}, {}

        def weave(dst, src, slots):
            nc.scalar.copy(dst[:, :, 0:slots], src.rearrange("p t c -> p c t")[:, :, 0:slots])

        def weave_x(b, slots):
            x_woven[b] = ring.tile([P, NP, 4], BF16, name="x_woven", align_bytes=64, bufs=3)
            weave(x_woven[b][:], x_bf[b][:], slots)

        def weave_page(b, h, slots):
            if h == 0:
                page_woven[b] = ring.tile([P, T2, 4], BF16, name="page_woven", align_bytes=64)
            cols = slice(512 * h, 512 * (h + 1))
            weave(page_woven[b][:, cols, :], page_bf[b][:, :, cols], slots)

        def quant_page(b, pieces):
            for h in range(pieces):
                cols = slice(T2 // pieces * h, T2 // pieces * (h + 1))
                nc.vector.quantize_mx(
                    page_c[b][:, cols].bitcast(FP8X4), page_s[b][:, cols], page_woven[b][:, cols, :].rearrange("p c t -> p (c t)")
                )

        def quant_x(b):
            tag = "after_last_scatter" if b == 1 else "x_c%d" % b
            x_c[b] = keep.tile([P, NP], U32, name="x_c", tag=tag, align_bytes=64)
            nc.vector.quantize_mx(x_c[b][:].bitcast(FP8X4), x_s[b][:], x_woven[b][:].rearrange("p c t -> p (c t)"))

        def scores(b):
            for m in range(T2 // P):
                if b == 0:
                    e_ps[m] = psum.tile([P, NP], F32, name="bank%d" % m)
                cols = slice(P * m, P * (m + 1))
                nc.tensor.matmul_mx(
                    e_ps[m][:], lhsT=page_c[b][:, cols].bitcast(FP8X4), lhsT_scale=page_s[b][:, cols],
                    rhs=x_c[b][:].bitcast(FP8X4), rhs_scale=x_s[b][:], start=(b == 0), stop=(b == PASSES - 1),
                )

        def put(k):
            pieces = 2 if k == 0 else 1
            for h in range(pieces):
                cols = slice(S // pieces * h, S // pieces * (h + 1))
                offsets = idx2[:, cols.start // 16 : cols.stop // 16]
                nc.vector.tensor_tensor(page_sb[k][:].indirect(offsets), shrink[k][:, cols], lot_sb[k][:, cols], ALU.mult)

        def pick(k):
            b, t = divmod(k, 4)
            shifted[k] = ring.tile([P, NP], F32, name="shifted", bufs=3)
            nc.vector.tensor_tensor(shifted[k][:], page_sb[k][:].indirect(idx3[:]), clean_sb[k][:], ALU.add)
            if k >= TILES - 2:
                nc.vector.tensor_scalar(x_woven[b][:, :, t], shifted[k][:], gv_sb[:, b, t : t + 1], None, ALU.mult)

        def round_page(k):
            b, t = divmod(k, 4)
            if t == 0:
                page_bf[b] = ring.tile([P, 4, T2], BF16, name="page_bf")
            if k < TILES - 1:
                nc.scalar.copy(page_bf[b][:, t, :], page_sb[k][:])
            else:
                for h in range(2):
                    cols = slice(512 * h, 512 * (h + 1))
                    nc.scalar.copy(page_woven[b][:, cols, t], page_sb[k][:, cols])

        def round_x(k):
            b, t = divmod(k, 4)
            if t == 0:
                x_bf[b] = ring.tile([P, 4, NP], BF16, name="x_bf")
            nc.scalar.activation(x_bf[b][:, t, :], shifted[k][:], ACT.Copy, scale=gv_sb[:, b, t : t + 1])

        for k in range(TILES):
            b, t = divmod(k, 4)
            if t == 0 and b + 1 < PASSES:
                weave_w1(b + 1, nc.scalar.copy)
                quant_w1(b + 1)
                for tile in range(4 * b + 4, 4 * b + 8):
                    readout(tile)
            put(k)
            if k + 1 < TILES:
                weigh(k + 1)
            else:
                quant_x(1)
                scores(1)
            if k == TILES - 2:
                weave_x(b, 2)
            pick(k)
            if k % 2 == 1 and k + 3 < TILES:
                chain(k + 3)
            if k < TILES - 1:
                round_page(k)
            if k < TILES - 2:
                round_x(k)
            if b > 0 and t == 0:
                for h in range(2):
                    weave_page(b - 1, h, 4)
            if b > 0 and t == 1:
                weave_x(b - 1, 4)
                quant_page(b - 1, 1)
            if k == 5:
                quant_x(0)
                scores(0)
            if k == TILES - 2:
                for h in range(2):
                    weave_page(b, h, 3)
        round_page(TILES - 1)
        quant_x(2)
        quant_page(2, 2)
        scores(2)

        for m in range(T2 // P):
            staged = ring.tile([P, NP], F32, name="staged", bufs=5)
            if m in (2, 5):
                nc.vector.tensor_scalar(staged[:], e_ps[m][:], slot_sb[:, m : m + 1], -1.0, ALU.subtract, ALU.mult)
                nc.vector.scalar_tensor_tensor(staged[:], staged[:], -1.0, staged[:], ALU.mult, ALU.max)
            else:
                nc.scalar.activation(staged[:], e_ps[m][:], ACT.Abs, bias=slot_sb[:, m : m + 1], scale=-1.0)
            nc.sync.dma_start(out[P * m : P * (m + 1), :], staged[:])
